import numpy as np
import ml_dtypes


def mxq(x, axis, fmt="e4m3"):
    dtype, down = {"e4m3": (ml_dtypes.float8_e4m3fn, 7), "e5m2": (ml_dtypes.float8_e5m2, 14)}[fmt]
    v = np.moveaxis(np.asarray(x, np.float32).astype(ml_dtypes.bfloat16).astype(np.float64), axis, -1)
    blocks = v.reshape(v.shape[:-1] + (-1, 32))
    amax = np.abs(blocks).max(-1, keepdims=True)
    byte = np.maximum(np.where(amax > 0, np.frexp(amax)[1] - 1 + 127, 0) - down, 1)
    scale = np.exp2(byte - 127.0)
    codes = (blocks / scale).astype(np.float32).astype(dtype).astype(np.float64)
    return np.moveaxis((codes * scale).reshape(v.shape), -1, axis)


WIDE = False


def mx_kscale(k):
    if not WIDE:
        return np.ones(k)
    levels = np.array([10, -10, 5, -5, 0])
    if k % 512:
        return np.exp2(np.random.permutation(np.resize(levels, k // 32))).repeat(32)
    a = np.empty((k // 512, 16))
    for p in range(k // 512):
        a[p, :8] = np.random.permutation(np.resize(levels, 8))
        for g in range(8):
            far = levels[np.abs(levels - a[p, g]) >= 10]
            a[p, g + 8] = far[np.random.randint(len(far))]
    return np.exp2(a.ravel()).repeat(32)


def f64(x):
    return np.asarray(x).astype(np.float64)


def striped(idx):
    return np.tile(idx.reshape(-1, 16).T, (8, 1)).astype(np.uint16)


def unstriped(offs):
    return offs[:16].T.reshape(-1).astype(np.int64)


def gelu(v):
    return 0.5 * v * (1.0 + np.tanh(np.sqrt(2.0 / np.pi) * (v + 0.044715 * v**3)))


K, T, E, C, N = 512, 512, 2, 256, 128


def by_expert(wq, xq):
    return np.concatenate([wq[e].T @ xq[:, e * C:(e + 1) * C] for e in range(E)], axis=1)


def setup_inputs():
    n = np.random.standard_normal
    s = mx_kscale(K)[:, None]
    return {
        "xT": (n((K, T)) * s).astype(np.float32),
        "w": (n((E, K, N)) / np.sqrt(K) / s[None]).astype(np.float32),
        "b": (0.3 * n((N, E))).astype(np.float32),
        "gate": np.tile(np.random.uniform(0.2, 1.0, E * C), (N, 1)).astype(np.float32),
        "offs": striped(np.random.permutation(T)[:E * C]),
    }


def reference(xT, w, b, gate, offs):
    idx = unstriped(offs)
    xq = mxq(f64(xT)[:, idx], 0, "e4m3")
    y = by_expert(mxq(f64(w), 1, "e4m3"), xq)
    y = gelu(y + np.repeat(f64(b), C, axis=1))
    out = np.zeros((N, T))
    out[:, idx] = f64(gate) * y
    return out

@@ -1,0 +1,157 @@
+from contextlib import ExitStack
+
+import concourse.mybir as mybir
+
+K, T, E, C, N = 512, 512, 2, 256, 128
+FLOPS = 2 * K * N * E * C
+
+F32 = mybir.dt.float32
+BF16 = mybir.dt.bfloat16
+U32 = mybir.dt.uint32
+U16 = mybir.dt.uint16
+U8 = mybir.dt.uint8
+FP8X4 = mybir.dt.float8_e4m3fn_x4
+GELU = mybir.ActivationFunctionType.Gelu_apprx_tanh
+MULT = mybir.AluOpType.mult
+
+P = 128
+PACK = 4
+SLOTS = E * C
+PIECE = 128
+
+
+def tile_routed_moe_kernel(tc, xT, w, b, gate, offs, out):
+    nc = tc.nc
+    with ExitStack() as ctx:
+        keep = ctx.enter_context(tc.tile_pool(name="keep", bufs=1))
+        psum = ctx.enter_context(tc.psum_pool(name="psum", bufs=1))
+
+        offsets = keep.tile([P, SLOTS // 16], U16, name="offsets")
+        nc.sync.dma_start(offsets[:], offs)
+
+        x_view = xT.rearrange("(p t) n -> p t n", t=PACK)
+        planes = [keep.tile([P, T], F32, name="plane%d" % t) for t in range(PACK)]
+        w_raw = [keep.tile([P, PACK, N], F32, name="w_raw%d" % e) for e in range(E)]
+        gate_sb = keep.tile([P, SLOTS], F32, name="gate_sb")
+        bias = keep.tile([P, E], F32, name="bias")
+
+        def load_plane(t):
+            nc.sync.dma_start(planes[t][:], x_view[:, t, :])
+
+        def load_w(e):
+            nc.sync.dma_start(w_raw[e][:], w[e].rearrange("(p j) n -> p j n", j=PACK))
+
+        load_plane(0)
+        load_plane(1)
+        load_w(0)
+        load_w(1)
+        load_plane(2)
+        nc.sync.dma_start(gate_sb[:], gate)
+        nc.sync.dma_start(bias[:], b)
+        load_plane(3)
+
+        warm_in = keep.tile([P, 1], F32, name="warm_in")
+        warm_out = keep.tile([P, 1], F32, name="warm_out")
+        nc.vector.memset(warm_in[:], 0.0)
+        nc.scalar.activation(out=warm_out[:], in_=warm_in[:], func=GELU)
+
+        w_grouped = keep.tile([P, E, N, PACK], BF16, name="w_grouped", align_bytes=64)
+        w_codes = keep.tile([P, E * N], U32, name="w_codes", align_bytes=64)
+        w_scales = keep.tile([P, E * N], U8, name="w_scales", align_bytes=64)
+        x_codes = keep.tile([P, SLOTS], U32, name="x_codes", align_bytes=64)
+        x_scales = keep.tile([P, SLOTS], U8, name="x_scales", align_bytes=64)
+        window = keep.tile([P, T], F32, name="window")
+        g4 = [keep.tile([P, PACK, C], F32, name="g4_%d" % e) for e in range(E)]
+
+        grouped = {}
+        results = {}
+
+        def gather(t, first, count):
+            e = first // C
+            nc.vector.tensor_copy(
+                g4[e][:, t, first - e * C : first - e * C + count],
+                planes[t][:].indirect(offsets[:, first // 16 : (first + count) // 16]),
+            )
+
+        def interleave(s):
+            e = s // C
+            grp = keep.tile([P, PIECE, PACK], BF16, name="grouped%d" % s, align_bytes=64)
+            nc.scalar.copy(
+                out=grp[:], in_=g4[e][:, :, s - e * C : s - e * C + PIECE].rearrange("p t n -> p n t")
+            )
+            grouped[s] = grp
+
+        def interleave_w(e):
+            nc.scalar.copy(out=w_grouped[:, e, :, :], in_=w_raw[e][:].rearrange("p j n -> p n j"))
+
+        def quantize_w():
+            nc.vector.quantize_mx(
+                out=w_codes[:].bitcast(FP8X4),
+                scales=w_scales[:],
+                in_=w_grouped[:].rearrange("p e n j -> p (e n j)"),
+            )
+
+        def quantize(s):
+            cols = slice(s, s + PIECE)
+            nc.vector.quantize_mx(
+                out=x_codes[:, cols].bitcast(FP8X4),
+                scales=x_scales[:, cols],
+                in_=grouped[s][:].rearrange("p n t -> p (n t)"),
+            )
+
+        def multiply(s):
+            e = s // C
+            cols = slice(s, s + PIECE)
+            acc = psum.tile([P, PIECE], F32, name="acc%d" % s)
+            nc.tensor.matmul_mx(
+                out=acc[:],
+                lhsT=w_codes[:, e * N : (e + 1) * N].bitcast(FP8X4),
+                lhsT_scale=w_scales[:, e * N : (e + 1) * N],
+                rhs=x_codes[:, cols].bitcast(FP8X4),
+                rhs_scale=x_scales[:, cols],
+                start=True,
+                stop=True,
+            )
+            y = keep.tile([P, PIECE], F32, name="y%d" % s)
+            nc.scalar.activation(out=y[:], in_=acc[:], func=GELU, bias=bias[:, e : e + 1], scale=1.0)
+            results[s] = y
+
+        def scatter(s):
+            nc.vector.tensor_tensor(
+                window[:].indirect(offsets[:, s // 16 : (s + PIECE) // 16]),
+                results[s][:],
+                gate_sb[:, s : s + PIECE],
+                MULT,
+            )
+
+        gather(0, 0, 256)
+        gather(0, 256, 256)
+        gather(1, 0, 256)
+        gather(1, 256, 256)
+        interleave_w(0)
+        interleave_w(1)
+        gather(2, 0, 256)
+        gather(2, 256, 256)
+        quantize_w()
+        gather(3, 0, 128)
+        interleave(0)
+        gather(3, 128, 128)
+        interleave(128)
+        gather(3, 256, 128)
+        quantize(0)
+        multiply(0)
+        interleave(256)
+        gather(3, 384, 128)
+        quantize(128)
+        multiply(128)
+        interleave(384)
+        scatter(0)
+        quantize(256)
+        multiply(256)
+        scatter(128)
+        quantize(384)
+        multiply(384)
+        scatter(256)
+        scatter(384)
+
+        nc.sync.dma_start(out, window[:])

@@ -117,11 +117,10 @@ def tile_routed_moe_kernel(tc, xT, w, b, gate, offs, out):
             results[s] = y
 
         def scatter(s):
-            nc.vector.tensor_tensor(
-                window[:].indirect(offsets[:, s // 16 : (s + PIECE) // 16]),
-                results[s][:],
-                gate_sb[:, s : s + PIECE],
-                MULT,
+            weighted = keep.tile([P, PIECE], F32, name="weighted%d" % s)
+            nc.vector.tensor_tensor(weighted[:], results[s][:], gate_sb[:, s : s + PIECE], MULT)
+            nc.vector.tensor_copy(
+                window[:].indirect(offsets[:, s // 16 : (s + PIECE) // 16]), weighted[:]
             )
 
         gather(0, 0, 256)

@@ -18,6 +18,8 @@ P = 128
 PACK = 4
 SLOTS = E * C
 PIECE = 128
+COPY = mybir.ActivationFunctionType.Copy
+ADD = mybir.AluOpType.add
 
 
 def tile_routed_moe_kernel(tc, xT, w, b, gate, offs, out):
@@ -44,11 +46,11 @@ def tile_routed_moe_kernel(tc, xT, w, b, gate, offs, out):
         load_plane(0)
         load_plane(1)
         load_w(0)
-        load_w(1)
         load_plane(2)
+        load_w(1)
+        load_plane(3)
         nc.sync.dma_start(gate_sb[:], gate)
         nc.sync.dma_start(bias[:], b)
-        load_plane(3)
 
         warm_in = keep.tile([P, 1], F32, name="warm_in")
         warm_out = keep.tile([P, 1], F32, name="warm_out")
@@ -61,25 +63,40 @@ def tile_routed_moe_kernel(tc, xT, w, b, gate, offs, out):
         x_codes = keep.tile([P, SLOTS], U32, name="x_codes", align_bytes=64)
         x_scales = keep.tile([P, SLOTS], U8, name="x_scales", align_bytes=64)
         window = keep.tile([P, T], F32, name="window")
-        g4 = [keep.tile([P, PACK, C], F32, name="g4_%d" % e) for e in range(E)]
+        g4 = keep.tile([P, PACK, SLOTS], F32, name="g4")
+        x_bf = keep.tile([P, PACK, T], BF16, name="x_bf", tag="swap", align_bytes=64)
+        grouped_d = keep.tile([P, PIECE, PACK], BF16, name="grouped_d", align_bytes=64)
+        grouped = {384: grouped_d[:]}
 
-        grouped = {}
+        def open_abc():
+            grouped_abc = keep.tile(
+                [P, 3 * PIECE, PACK], BF16, name="grouped_abc", tag="swap", align_bytes=64
+            )
+            for s in range(0, 3 * PIECE, PIECE):
+                grouped[s] = grouped_abc[:, s : s + PIECE, :]
+
         results = {}
 
+        def cast(t):
+            nc.gpsimd.tensor_scalar(
+                out=x_bf[:, t, :], in0=planes[t][:], scalar1=1.0, scalar2=0.0, op0=MULT, op1=ADD
+            )
+
         def gather(t, first, count):
-            e = first // C
             nc.vector.tensor_copy(
-                g4[e][:, t, first - e * C : first - e * C + count],
+                g4[:, t, first : first + count],
                 planes[t][:].indirect(offsets[:, first // 16 : (first + count) // 16]),
             )
 
-        def interleave(s):
-            e = s // C
-            grp = keep.tile([P, PIECE, PACK], BF16, name="grouped%d" % s, align_bytes=64)
-            nc.scalar.copy(
-                out=grp[:], in_=g4[e][:, :, s - e * C : s - e * C + PIECE].rearrange("p t n -> p n t")
+        def gather_scalar(t, s):
+            nc.scalar.activation(
+                out=grouped[s][:, :, t],
+                in_=x_bf[:, t, :].indirect(offsets[:, s // 16 : (s + PIECE) // 16]),
+                func=COPY,
             )
-            grouped[s] = grp
+
+        def interleave(s):
+            nc.scalar.copy(out=grouped[s], in_=g4[:, :, s : s + PIECE].rearrange("p t n -> p n t"))
 
         def interleave_w(e):
             nc.scalar.copy(out=w_grouped[:, e, :, :], in_=w_raw[e][:].rearrange("p j n -> p n j"))
@@ -96,7 +113,7 @@ def tile_routed_moe_kernel(tc, xT, w, b, gate, offs, out):
             nc.vector.quantize_mx(
                 out=x_codes[:, cols].bitcast(FP8X4),
                 scales=x_scales[:, cols],
-                in_=grouped[s][:].rearrange("p n t -> p (n t)"),
+                in_=grouped[s].rearrange("p n t -> p (n t)"),
             )
 
         def multiply(s):
@@ -117,40 +134,48 @@ def tile_routed_moe_kernel(tc, xT, w, b, gate, offs, out):
             results[s] = y
 
         def scatter(s):
-            weighted = keep.tile([P, PIECE], F32, name="weighted%d" % s)
-            nc.vector.tensor_tensor(weighted[:], results[s][:], gate_sb[:, s : s + PIECE], MULT)
-            nc.vector.tensor_copy(
-                window[:].indirect(offsets[:, s // 16 : (s + PIECE) // 16]), weighted[:]
+            nc.vector.tensor_tensor(
+                window[:].indirect(offsets[:, s // 16 : (s + PIECE) // 16]),
+                results[s][:],
+                gate_sb[:, s : s + PIECE],
+                MULT,
             )
 
+        cast(0)
         gather(0, 0, 256)
-        gather(0, 256, 256)
+        gather(0, 256, 128)
+        gather_scalar(0, 384)
+        cast(1)
         gather(1, 0, 256)
-        gather(1, 256, 256)
+        gather(1, 256, 128)
+        gather_scalar(1, 384)
         interleave_w(0)
-        interleave_w(1)
+        cast(2)
         gather(2, 0, 256)
-        gather(2, 256, 256)
+        gather(2, 256, 128)
+        gather_scalar(2, 384)
+        interleave_w(1)
         quantize_w()
+        cast(3)
         gather(3, 0, 128)
-        interleave(0)
         gather(3, 128, 128)
-        interleave(128)
         gather(3, 256, 128)
+        gather_scalar(3, 384)
+        open_abc()
+        quantize(384)
+        multiply(384)
+        interleave(0)
         quantize(0)
         multiply(0)
-        interleave(256)
-        gather(3, 384, 128)
+        scatter(384)
+        interleave(128)
         quantize(128)
         multiply(128)
-        interleave(384)
         scatter(0)
+        interleave(256)
         quantize(256)
         multiply(256)
         scatter(128)
-        quantize(384)
-        multiply(384)
         scatter(256)
-        scatter(384)
 
         nc.sync.dma_start(out, window[:])

@@ -96,10 +96,16 @@ def tile_routed_moe_kernel(tc, xT, w, b, gate, offs, out):
             )
 
         def interleave(s):
-            nc.scalar.copy(out=grouped[s], in_=g4[:, :, s : s + PIECE].rearrange("p t n -> p n t"))
+            nc.scalar.copy(
+                out=grouped[s].rearrange("p (c i) t -> p c t i", i=4),
+                in_=g4[:, :, s : s + PIECE].rearrange("p t (c i) -> p c t i", i=4),
+            )
 
         def interleave_w(e):
-            nc.scalar.copy(out=w_grouped[:, e, :, :], in_=w_raw[e][:].rearrange("p j n -> p n j"))
+            nc.scalar.copy(
+                out=w_grouped[:, e, :, :].rearrange("p (c i) j -> p c j i", i=4),
+                in_=w_raw[e][:].rearrange("p j (c i) -> p c j i", i=4),
+            )
 
         def quantize_w():
             nc.vector.quantize_mx(
@@ -142,17 +148,14 @@ def tile_routed_moe_kernel(tc, xT, w, b, gate, offs, out):
             )
 
         cast(0)
-        gather(0, 0, 256)
-        gather(0, 256, 128)
+        gather(0, 0, 384)
         gather_scalar(0, 384)
         cast(1)
-        gather(1, 0, 256)
-        gather(1, 256, 128)
+        gather(1, 0, 384)
         gather_scalar(1, 384)
         interleave_w(0)
         cast(2)
-        gather(2, 0, 256)
-        gather(2, 256, 128)
+        gather(2, 0, 384)
         gather_scalar(2, 384)
         interleave_w(1)
         quantize_w()

@@ -21,6 +21,8 @@ PIECE = 128
 COPY = mybir.ActivationFunctionType.Copy
 ADD = mybir.AluOpType.add
 
+VEC = 256
+
 
 def tile_routed_moe_kernel(tc, xT, w, b, gate, offs, out):
     nc = tc.nc
@@ -43,43 +45,50 @@ def tile_routed_moe_kernel(tc, xT, w, b, gate, offs, out):
         def load_w(e):
             nc.sync.dma_start(w_raw[e][:], w[e].rearrange("(p j) n -> p j n", j=PACK))
 
+        def load_gate():
+            nc.sync.dma_start(gate_sb[:], gate)
+
+        def load_bias():
+            nc.sync.dma_start(bias[:], b)
+
         load_plane(0)
         load_plane(1)
-        load_w(0)
         load_plane(2)
-        load_w(1)
         load_plane(3)
-        nc.sync.dma_start(gate_sb[:], gate)
-        nc.sync.dma_start(bias[:], b)
+        load_w(0)
+        load_w(1)
+        load_gate()
+        load_bias()
 
         warm_in = keep.tile([P, 1], F32, name="warm_in")
         warm_out = keep.tile([P, 1], F32, name="warm_out")
         nc.vector.memset(warm_in[:], 0.0)
         nc.scalar.activation(out=warm_out[:], in_=warm_in[:], func=GELU)
 
-        w_grouped = keep.tile([P, E, N, PACK], BF16, name="w_grouped", align_bytes=64)
-        w_codes = keep.tile([P, E * N], U32, name="w_codes", align_bytes=64)
-        w_scales = keep.tile([P, E * N], U8, name="w_scales", align_bytes=64)
-        x_codes = keep.tile([P, SLOTS], U32, name="x_codes", align_bytes=64)
-        x_scales = keep.tile([P, SLOTS], U8, name="x_scales", align_bytes=64)
+        w_grouped = [
+            keep.tile([P, N, PACK], BF16, name="w_grouped%d" % e, align_bytes=64) for e in range(E)
+        ]
+        w_codes = [keep.tile([P, N], U32, name="w_codes%d" % e, align_bytes=64) for e in range(E)]
+        w_scales = [keep.tile([P, N], U8, name="w_scales%d" % e, align_bytes=64) for e in range(E)]
         window = keep.tile([P, T], F32, name="window")
-        g4 = keep.tile([P, PACK, SLOTS], F32, name="g4")
-        x_bf = keep.tile([P, PACK, T], BF16, name="x_bf", tag="swap", align_bytes=64)
-        grouped_d = keep.tile([P, PIECE, PACK], BF16, name="grouped_d", align_bytes=64)
-        grouped = {384: grouped_d[:]}
-
-        def open_abc():
-            grouped_abc = keep.tile(
-                [P, 3 * PIECE, PACK], BF16, name="grouped_abc", tag="swap", align_bytes=64
-            )
-            for s in range(0, 3 * PIECE, PIECE):
-                grouped[s] = grouped_abc[:, s : s + PIECE, :]
-
+        g4 = keep.tile([P, PACK, VEC], F32, name="g4")
+        x_bf = [
+            keep.tile([P, T], BF16, name="x_bf%d" % t, tag="swap%d" % t, align_bytes=64)
+            for t in range(PACK)
+        ]
+        grouped = {}
+        x_codes = {}
+        x_scales = {}
         results = {}
+
+        def open_piece(s, count, tag):
+            grouped[s] = keep.tile([P, count, PACK], BF16, name="grouped%d" % s, tag=tag, align_bytes=64)
+            x_codes[s] = keep.tile([P, count], U32, name="x_codes%d" % s, align_bytes=64)
+            x_scales[s] = keep.tile([P, count], U8, name="x_scales%d" % s, align_bytes=64)
 
         def cast(t):
             nc.gpsimd.tensor_scalar(
-                out=x_bf[:, t, :], in0=planes[t][:], scalar1=1.0, scalar2=0.0, op0=MULT, op1=ADD
+                out=x_bf[t][:], in0=planes[t][:], scalar1=1.0, scalar2=0.0, op0=MULT, op1=ADD
             )
 
         def gather(t, first, count):
@@ -88,97 +97,122 @@ def tile_routed_moe_kernel(tc, xT, w, b, gate, offs, out):
                 planes[t][:].indirect(offsets[:, first // 16 : (first + count) // 16]),
             )
 
-        def gather_scalar(t, s):
+        def gather_scalar(t, s, first, count):
             nc.scalar.activation(
-                out=grouped[s][:, :, t],
-                in_=x_bf[:, t, :].indirect(offsets[:, s // 16 : (s + PIECE) // 16]),
+                out=grouped[s][:, first - s : first - s + count, t],
+                in_=x_bf[t][:].indirect(offsets[:, first // 16 : (first + count) // 16]),
                 func=COPY,
             )
 
-        def interleave(s):
+        def interleave(s, count):
             nc.scalar.copy(
-                out=grouped[s].rearrange("p (c i) t -> p c t i", i=4),
-                in_=g4[:, :, s : s + PIECE].rearrange("p t (c i) -> p c t i", i=4),
+                out=grouped[s][:].rearrange("p (c i) t -> p c t i", i=4),
+                in_=g4[:, :, s : s + count].rearrange("p t (c i) -> p c t i", i=4),
+            )
+
+        def interleave_vector(s, count):
+            nc.vector.tensor_copy(
+                out=grouped[s][:].rearrange("p (c i) t -> p c t i", i=4),
+                in_=g4[:, :, s : s + count].rearrange("p t (c i) -> p c t i", i=4),
             )
 
         def interleave_w(e):
             nc.scalar.copy(
-                out=w_grouped[:, e, :, :].rearrange("p (c i) j -> p c j i", i=4),
+                out=w_grouped[e][:].rearrange("p (c i) j -> p c j i", i=4),
                 in_=w_raw[e][:].rearrange("p j (c i) -> p c j i", i=4),
             )
 
-        def quantize_w():
-            nc.vector.quantize_mx(
-                out=w_codes[:].bitcast(FP8X4),
-                scales=w_scales[:],
-                in_=w_grouped[:].rearrange("p e n j -> p (e n j)"),
+        def interleave_w_pool(e):
+            nc.gpsimd.tensor_scalar(
+                out=w_grouped[e][:],
+                in0=w_raw[e][:].rearrange("p j n -> p n j"),
+                scalar1=1.0,
+                scalar2=0.0,
+                op0=MULT,
+                op1=ADD,
             )
 
-        def quantize(s):
-            cols = slice(s, s + PIECE)
-            nc.vector.quantize_mx(
-                out=x_codes[:, cols].bitcast(FP8X4),
-                scales=x_scales[:, cols],
-                in_=grouped[s].rearrange("p n t -> p (n t)"),
+        def interleave_w_vector(e):
+            nc.vector.tensor_copy(
+                out=w_grouped[e][:].rearrange("p (c i) j -> p c j i", i=4),
+                in_=w_raw[e][:].rearrange("p j (c i) -> p c j i", i=4),
             )
 
-        def multiply(s):
-            e = s // C
-            cols = slice(s, s + PIECE)
-            acc = psum.tile([P, PIECE], F32, name="acc%d" % s)
+        def quantize_w(e):
+            nc.vector.quantize_mx(
+                out=w_codes[e][:].bitcast(FP8X4),
+                scales=w_scales[e][:],
+                in_=w_grouped[e][:].rearrange("p n j -> p (n j)"),
+            )
+
+        def quantize(s, first, count):
+            cols = slice(first - s, first - s + count)
+            nc.vector.quantize_mx(
+                out=x_codes[s][:, cols].bitcast(FP8X4),
+                scales=x_scales[s][:, cols],
+                in_=grouped[s][:, cols, :].rearrange("p n t -> p (n t)"),
+            )
+
+        def multiply(s, first, count):
+            e = first // C
+            cols = slice(first - s, first - s + count)
+            acc = psum.tile([P, count], F32, name="acc%d" % first)
             nc.tensor.matmul_mx(
                 out=acc[:],
-                lhsT=w_codes[:, e * N : (e + 1) * N].bitcast(FP8X4),
-                lhsT_scale=w_scales[:, e * N : (e + 1) * N],
-                rhs=x_codes[:, cols].bitcast(FP8X4),
-                rhs_scale=x_scales[:, cols],
+                lhsT=w_codes[e][:].bitcast(FP8X4),
+                lhsT_scale=w_scales[e][:],
+                rhs=x_codes[s][:, cols].bitcast(FP8X4),
+                rhs_scale=x_scales[s][:, cols],
                 start=True,
                 stop=True,
             )
-            y = keep.tile([P, PIECE], F32, name="y%d" % s)
+            y = keep.tile([P, count], F32, name="y%d" % first)
             nc.scalar.activation(out=y[:], in_=acc[:], func=GELU, bias=bias[:, e : e + 1], scale=1.0)
-            results[s] = y
+            results[first] = y
 
-        def scatter(s):
+        def scatter(first, count):
             nc.vector.tensor_tensor(
-                window[:].indirect(offsets[:, s // 16 : (s + PIECE) // 16]),
-                results[s][:],
-                gate_sb[:, s : s + PIECE],
+                window[:].indirect(offsets[:, first // 16 : (first + count) // 16]),
+                results[first][:],
+                gate_sb[:, first : first + count],
                 MULT,
             )
 
+        open_piece(256, 256, "grouped256")
         cast(0)
-        gather(0, 0, 384)
-        gather_scalar(0, 384)
+        gather(0, 0, VEC)
+        gather_scalar(0, 256, 256, 256)
         cast(1)
-        gather(1, 0, 384)
-        gather_scalar(1, 384)
-        interleave_w(0)
+        gather(1, 0, VEC)
+        gather_scalar(1, 256, 256, 256)
         cast(2)
-        gather(2, 0, 384)
-        gather_scalar(2, 384)
-        interleave_w(1)
-        quantize_w()
-        cast(3)
+        gather(2, 0, VEC)
         gather(3, 0, 128)
         gather(3, 128, 128)
-        gather(3, 256, 128)
-        gather_scalar(3, 384)
-        open_abc()
-        quantize(384)
-        multiply(384)
-        interleave(0)
-        quantize(0)
-        multiply(0)
-        scatter(384)
-        interleave(128)
-        quantize(128)
-        multiply(128)
-        scatter(0)
-        interleave(256)
-        quantize(256)
-        multiply(256)
-        scatter(128)
-        scatter(256)
+        interleave_w_pool(0)
+        cast(3)
+        open_piece(0, 128, "swap0")
+        open_piece(128, 128, "grouped128")
+        interleave(0, 128)
+        interleave_vector(128, 128)
+        quantize_w(0)
+        quantize(0, 0, 128)
+        multiply(0, 0, 128)
+        quantize(128, 128, 128)
+        multiply(128, 128, 128)
+        scatter(0, 128)
+        gather_scalar(2, 256, 256, 128)
+        gather_scalar(3, 256, 256, 128)
+        interleave_w_pool(1)
+        quantize_w(1)
+        quantize(256, 256, 128)
+        multiply(256, 256, 128)
+        scatter(128, 128)
+        gather_scalar(2, 256, 384, 128)
+        gather_scalar(3, 256, 384, 128)
+        quantize(256, 384, 128)
+        multiply(256, 384, 128)
+        scatter(256, 128)
+        scatter(384, 128)
 
         nc.sync.dma_start(out, window[:])

@@ -66,7 +66,7 @@ def tile_routed_moe_kernel(tc, xT, w, b, gate, offs, out):
         nc.scalar.activation(out=warm_out[:], in_=warm_in[:], func=GELU)
 
         w_grouped = [
-            keep.tile([P, N, PACK], BF16, name="w_grouped%d" % e, align_bytes=64) for e in range(E)
+            keep.tile([P, N, PACK], BF16, name="w_grouped%d" % e, align_bytes=64) for e in range(0)
         ]
         w_codes = [keep.tile([P, N], U32, name="w_codes%d" % e, align_bytes=64) for e in range(E)]
         w_scales = [keep.tile([P, N], U8, name="w_scales%d" % e, align_bytes=64) for e in range(E)]
@@ -81,9 +81,16 @@ def tile_routed_moe_kernel(tc, xT, w, b, gate, offs, out):
         x_scales = {}
         results = {}
 
+        def open_w(tag):
+            w_grouped.append(
+                keep.tile([P, N, PACK], BF16, name="w_grouped%d" % len(w_grouped), tag=tag, align_bytes=64)
+            )
+
         def open_piece(s, count, tag):
             grouped[s] = keep.tile([P, count, PACK], BF16, name="grouped%d" % s, tag=tag, align_bytes=64)
-            x_codes[s] = keep.tile([P, count], U32, name="x_codes%d" % s, align_bytes=64)
+
+        def open_codes(s, count, tag):
+            x_codes[s] = keep.tile([P, count], U32, name="x_codes%d" % s, tag=tag, align_bytes=64)
             x_scales[s] = keep.tile([P, count], U8, name="x_scales%d" % s, align_bytes=64)
 
         def cast(t):
@@ -153,7 +160,7 @@ def tile_routed_moe_kernel(tc, xT, w, b, gate, offs, out):
                 in_=grouped[s][:, cols, :].rearrange("p n t -> p (n t)"),
             )
 
-        def multiply(s, first, count):
+        def multiply(s, first, count, tag):
             e = first // C
             cols = slice(first - s, first - s + count)
             acc = psum.tile([P, count], F32, name="acc%d" % first)
@@ -166,7 +173,7 @@ def tile_routed_moe_kernel(tc, xT, w, b, gate, offs, out):
                 start=True,
                 stop=True,
             )
-            y = keep.tile([P, count], F32, name="y%d" % first)
+            y = keep.tile([P, count], F32, name="y%d" % first, tag=tag, align_bytes=64)
             nc.scalar.activation(out=y[:], in_=acc[:], func=GELU, bias=bias[:, e : e + 1], scale=1.0)
             results[first] = y
 
@@ -187,32 +194,25 @@ def tile_routed_moe_kernel(tc, xT, w, b, gate, offs, out):
         gather_scalar(1, 256, 256, 256)
         cast(2)
         gather(2, 0, VEC)
-        gather(3, 0, 128)
-        gather(3, 128, 128)
-        interleave_w_pool(0)
+        gather_scalar(2, 256, 256, 256)
         cast(3)
-        open_piece(0, 128, "swap0")
-        open_piece(128, 128, "grouped128")
-        interleave(0, 128)
-        interleave_vector(128, 128)
-        quantize_w(0)
-        quantize(0, 0, 128)
-        multiply(0, 0, 128)
-        quantize(128, 128, 128)
-        multiply(128, 128, 128)
-        scatter(0, 128)
-        gather_scalar(2, 256, 256, 128)
-        gather_scalar(3, 256, 256, 128)
+        gather(3, 0, VEC)
+        gather_scalar(3, 256, 256, 256)
+        open_w("w_grouped0")
+        open_w("w_grouped1")
+        interleave_w_pool(0)
         interleave_w_pool(1)
+        open_piece(0, 256, "grouped0")
+        open_codes(0, 256, "x_codes0")
+        interleave_vector(0, 256)
+        quantize(0, 0, 256)
+        quantize_w(0)
+        multiply(0, 0, 256, "y0")
+        open_codes(256, 256, "w_grouped0")
+        quantize(256, 256, 256)
         quantize_w(1)
-        quantize(256, 256, 128)
-        multiply(256, 256, 128)
-        scatter(128, 128)
-        gather_scalar(2, 256, 384, 128)
-        gather_scalar(3, 256, 384, 128)
-        quantize(256, 384, 128)
-        multiply(256, 384, 128)
-        scatter(256, 128)
-        scatter(384, 128)
+        multiply(256, 256, 256, "y256")
+        scatter(0, 256)
+        scatter(256, 256)
 
         nc.sync.dma_start(out, window[:])

@@ -200,15 +200,15 @@ def tile_routed_moe_kernel(tc, xT, w, b, gate, offs, out):
         gather_scalar(3, 256, 256, 256)
         open_w("w_grouped0")
         open_w("w_grouped1")
-        interleave_w_pool(0)
-        interleave_w_pool(1)
         open_piece(0, 256, "grouped0")
         open_codes(0, 256, "x_codes0")
         interleave_vector(0, 256)
+        interleave_w_vector(0)
         quantize(0, 0, 256)
         quantize_w(0)
-        multiply(0, 0, 256, "y0")
-        open_codes(256, 256, "w_grouped0")
+        multiply(0, 0, 256, "swap3")
+        interleave_w_vector(1)
+        open_codes(256, 256, "x_codes256")
         quantize(256, 256, 256)
         quantize_w(1)
         multiply(256, 256, 256, "y256")

@@ -113,20 +113,20 @@ def tile_routed_moe_kernel(tc, xT, w, b, gate, offs, out):
 
         def interleave(s, count):
             nc.scalar.copy(
-                out=grouped[s][:].rearrange("p (c i) t -> p c t i", i=4),
-                in_=g4[:, :, s : s + count].rearrange("p t (c i) -> p c t i", i=4),
+                out=grouped[s][:].rearrange("p (c i) t -> p c t i", i=8),
+                in_=g4[:, :, s : s + count].rearrange("p t (c i) -> p c t i", i=8),
             )
 
         def interleave_vector(s, count):
             nc.vector.tensor_copy(
-                out=grouped[s][:].rearrange("p (c i) t -> p c t i", i=4),
-                in_=g4[:, :, s : s + count].rearrange("p t (c i) -> p c t i", i=4),
+                out=grouped[s][:].rearrange("p (c i) t -> p c t i", i=8),
+                in_=g4[:, :, s : s + count].rearrange("p t (c i) -> p c t i", i=8),
             )
 
         def interleave_w(e):
             nc.scalar.copy(
-                out=w_grouped[e][:].rearrange("p (c i) j -> p c j i", i=4),
-                in_=w_raw[e][:].rearrange("p j (c i) -> p c j i", i=4),
+                out=w_grouped[e][:].rearrange("p (c i) j -> p c j i", i=8),
+                in_=w_raw[e][:].rearrange("p j (c i) -> p c j i", i=8),
             )
 
         def interleave_w_pool(e):
@@ -141,8 +141,8 @@ def tile_routed_moe_kernel(tc, xT, w, b, gate, offs, out):
 
         def interleave_w_vector(e):
             nc.vector.tensor_copy(
-                out=w_grouped[e][:].rearrange("p (c i) j -> p c j i", i=4),
-                in_=w_raw[e][:].rearrange("p j (c i) -> p c j i", i=4),
+                out=w_grouped[e][:].rearrange("p (c i) j -> p c j i", i=8),
+                in_=w_raw[e][:].rearrange("p j (c i) -> p c j i", i=8),
             )
 
         def quantize_w(e):

@@ -117,10 +117,10 @@ def tile_routed_moe_kernel(tc, xT, w, b, gate, offs, out):
                 in_=g4[:, :, s : s + count].rearrange("p t (c i) -> p c t i", i=8),
             )
 
-        def interleave_vector(s, count):
+        def interleave_vector(s, first, count):
             nc.vector.tensor_copy(
-                out=grouped[s][:].rearrange("p (c i) t -> p c t i", i=8),
-                in_=g4[:, :, s : s + count].rearrange("p t (c i) -> p c t i", i=8),
+                out=grouped[s][:, first - s : first - s + count, :].rearrange("p (c i) t -> p c t i", i=8),
+                in_=g4[:, :, first : first + count].rearrange("p t (c i) -> p c t i", i=8),
             )
 
         def interleave_w(e):
@@ -173,9 +173,11 @@ def tile_routed_moe_kernel(tc, xT, w, b, gate, offs, out):
                 start=True,
                 stop=True,
             )
-            y = keep.tile([P, count], F32, name="y%d" % first, tag=tag, align_bytes=64)
-            nc.scalar.activation(out=y[:], in_=acc[:], func=GELU, bias=bias[:, e : e + 1], scale=1.0)
-            results[first] = y
+            if s not in results:
+                results[s] = keep.tile([P, 256], F32, name="y%d" % s, tag=tag, align_bytes=64)
+            nc.scalar.activation(
+                out=results[s][:, cols], in_=acc[:], func=GELU, bias=bias[:, e : e + 1], scale=1.0
+            )
 
         def scatter(first, count):
             nc.vector.tensor_tensor(
@@ -202,11 +204,14 @@ def tile_routed_moe_kernel(tc, xT, w, b, gate, offs, out):
         open_w("w_grouped1")
         open_piece(0, 256, "grouped0")
         open_codes(0, 256, "x_codes0")
-        interleave_vector(0, 256)
         interleave_w_vector(0)
-        quantize(0, 0, 256)
+        interleave_vector(0, 0, 128)
+        interleave_vector(0, 128, 128)
         quantize_w(0)
-        multiply(0, 0, 256, "swap3")
+        quantize(0, 0, 128)
+        quantize(0, 128, 128)
+        multiply(0, 0, 128, "swap3")
+        multiply(0, 128, 128, "swap3")
         interleave_w_vector(1)
         open_codes(256, 256, "x_codes256")
         quantize(256, 256, 256)

@@ -71,7 +71,8 @@ def tile_routed_moe_kernel(tc, xT, w, b, gate, offs, out):
         w_codes = [keep.tile([P, N], U32, name="w_codes%d" % e, align_bytes=64) for e in range(E)]
         w_scales = [keep.tile([P, N], U8, name="w_scales%d" % e, align_bytes=64) for e in range(E)]
         window = keep.tile([P, T], F32, name="window")
-        g4 = keep.tile([P, PACK, VEC], F32, name="g4")
+        pairs = keep.tile([P, 2, VEC, 2], BF16, name="pairs", align_bytes=64)
+        pair_words = pairs[:].rearrange("p u n e -> p (u n e)").bitcast(F32).rearrange("p (u n) -> p u n", u=2)
         x_bf = [
             keep.tile([P, T], BF16, name="x_bf%d" % t, tag="swap%d" % t, align_bytes=64)
             for t in range(PACK)
@@ -100,7 +101,7 @@ def tile_routed_moe_kernel(tc, xT, w, b, gate, offs, out):
 
         def gather(t, first, count):
             nc.vector.tensor_copy(
-                g4[:, t, first : first + count],
+                pairs[:, t // 2, first : first + count, t % 2],
                 planes[t][:].indirect(offsets[:, first // 16 : (first + count) // 16]),
             )
 
@@ -111,16 +112,11 @@ def tile_routed_moe_kernel(tc, xT, w, b, gate, offs, out):
                 func=COPY,
             )
 
-        def interleave(s, count):
-            nc.scalar.copy(
-                out=grouped[s][:].rearrange("p (c i) t -> p c t i", i=8),
-                in_=g4[:, :, s : s + count].rearrange("p t (c i) -> p c t i", i=8),
-            )
-
         def interleave_vector(s, first, count):
+            words = grouped[s][:].rearrange("p n t -> p (n t)").bitcast(F32)
             nc.vector.tensor_copy(
-                out=grouped[s][:, first - s : first - s + count, :].rearrange("p (c i) t -> p c t i", i=8),
-                in_=g4[:, :, first : first + count].rearrange("p t (c i) -> p c t i", i=8),
+                out=words[:, 2 * (first - s) : 2 * (first - s + count)].rearrange("p (c i u) -> p c u i", i=8, u=2),
+                in_=pair_words[:, :, first : first + count].rearrange("p u (c i) -> p c u i", i=8),
             )
 
         def interleave_w(e):

@@ -28,6 +28,7 @@ def tile_routed_moe_kernel(tc, xT, w, b, gate, offs, out):
     nc = tc.nc
     with ExitStack() as ctx:
         keep = ctx.enter_context(tc.tile_pool(name="keep", bufs=1))
+        shared = ctx.enter_context(tc.tile_pool(name="shared", bufs=1))
         psum = ctx.enter_context(tc.psum_pool(name="psum", bufs=1))
 
         offsets = keep.tile([P, SLOTS // 16], U16, name="offsets")
@@ -68,14 +69,15 @@ def tile_routed_moe_kernel(tc, xT, w, b, gate, offs, out):
         w_grouped = [
             keep.tile([P, N, PACK], BF16, name="w_grouped%d" % e, align_bytes=64) for e in range(0)
         ]
-        w_codes = [keep.tile([P, N], U32, name="w_codes%d" % e, align_bytes=64) for e in range(E)]
+        w_codes = []
         w_scales = [keep.tile([P, N], U8, name="w_scales%d" % e, align_bytes=64) for e in range(E)]
         window = keep.tile([P, T], F32, name="window")
         pairs = keep.tile([P, 2, VEC, 2], BF16, name="pairs", align_bytes=64)
         pair_words = pairs[:].rearrange("p u n e -> p (u n e)").bitcast(F32).rearrange("p (u n) -> p u n", u=2)
-        x_bf = [
+        x_bf = [shared.tile([P, T], BF16, name="x_bf0", offset=2048, align_bytes=64)]
+        x_bf += [
             keep.tile([P, T], BF16, name="x_bf%d" % t, tag="swap%d" % t, align_bytes=64)
-            for t in range(PACK)
+            for t in range(1, PACK)
         ]
         grouped = {}
         x_codes = {}
@@ -170,7 +172,7 @@ def tile_routed_moe_kernel(tc, xT, w, b, gate, offs, out):
                 stop=True,
             )
             if s not in results:
-                results[s] = keep.tile([P, 256], F32, name="y%d" % s, tag=tag, align_bytes=64)
+                results[s] = keep.tile([P, 256], F32, name="y%d" % s, tag=tag)
             nc.scalar.activation(
                 out=results[s][:, cols], in_=acc[:], func=GELU, bias=bias[:, e : e + 1], scale=1.0
             )
@@ -194,11 +196,14 @@ def tile_routed_moe_kernel(tc, xT, w, b, gate, offs, out):
         gather(2, 0, VEC)
         gather_scalar(2, 256, 256, 256)
         cast(3)
-        gather(3, 0, VEC)
+        gather(3, 0, 128)
+        gather(3, 128, 128)
         gather_scalar(3, 256, 256, 256)
         open_w("w_grouped0")
-        open_w("w_grouped1")
-        open_piece(0, 256, "grouped0")
+        grouped[0] = shared.tile([P, 256, PACK], BF16, name="grouped0", offset=64, align_bytes=64)
+        w_codes.append(shared.tile([P, N], U32, name="w_codes0", offset=2112, align_bytes=64))
+        w_codes.append(keep.tile([P, N], U32, name="w_codes1", align_bytes=64))
+        w_grouped.append(shared.tile([P, N, PACK], BF16, name="w_grouped1", offset=2624, align_bytes=64))
         open_codes(0, 256, "x_codes0")
         interleave_w_vector(0)
         interleave_vector(0, 0, 128)
@@ -206,8 +211,8 @@ def tile_routed_moe_kernel(tc, xT, w, b, gate, offs, out):
         quantize_w(0)
         quantize(0, 0, 128)
         quantize(0, 128, 128)
-        multiply(0, 0, 128, "swap3")
-        multiply(0, 128, 128, "swap3")
+        multiply(0, 0, 128, "plane3")
+        multiply(0, 128, 128, "plane3")
         interleave_w_vector(1)
         open_codes(256, 256, "x_codes256")
         quantize(256, 256, 256)

@@ -32,7 +32,6 @@ def tile_routed_moe_kernel(tc, xT, w, b, gate, offs, out):
         psum = ctx.enter_context(tc.psum_pool(name="psum", bufs=1))
 
         offsets = keep.tile([P, SLOTS // 16], U16, name="offsets")
-        nc.sync.dma_start(offsets[:], offs)
 
         x_view = xT.rearrange("(p t) n -> p t n", t=PACK)
         planes = [keep.tile([P, T], F32, name="plane%d" % t) for t in range(PACK)]
@@ -53,13 +52,14 @@ def tile_routed_moe_kernel(tc, xT, w, b, gate, offs, out):
             nc.sync.dma_start(bias[:], b)
 
         load_plane(0)
+        nc.sync.dma_start(offsets[:], offs)
         load_plane(1)
         load_plane(2)
         load_plane(3)
         load_w(0)
+        load_bias()
         load_w(1)
         load_gate()
-        load_bias()
 
         warm_in = keep.tile([P, 1], F32, name="warm_in")
         warm_out = keep.tile([P, 1], F32, name="warm_out")
@@ -96,9 +96,9 @@ def tile_routed_moe_kernel(tc, xT, w, b, gate, offs, out):
             x_codes[s] = keep.tile([P, count], U32, name="x_codes%d" % s, tag=tag, align_bytes=64)
             x_scales[s] = keep.tile([P, count], U8, name="x_scales%d" % s, align_bytes=64)
 
-        def cast(t):
+        def cast(t, first=0):
             nc.gpsimd.tensor_scalar(
-                out=x_bf[t][:], in0=planes[t][:], scalar1=1.0, scalar2=0.0, op0=MULT, op1=ADD
+                out=x_bf[t][:, first:], in0=planes[t][:, first:], scalar1=1.0, scalar2=0.0, op0=MULT, op1=ADD
             )
 
         def gather(t, first, count):
@@ -186,7 +186,8 @@ def tile_routed_moe_kernel(tc, xT, w, b, gate, offs, out):
             )
 
         open_piece(256, 256, "grouped256")
-        cast(0)
+        nc.scalar.copy(out=x_bf[0][:, : T // 2], in_=planes[0][:, : T // 2])
+        cast(0, T // 2)
         gather(0, 0, VEC)
         gather_scalar(0, 256, 256, 256)
         cast(1)
@@ -196,8 +197,7 @@ def tile_routed_moe_kernel(tc, xT, w, b, gate, offs, out):
         gather(2, 0, VEC)
         gather_scalar(2, 256, 256, 256)
         cast(3)
-        gather(3, 0, 128)
-        gather(3, 128, 128)
+        gather(3, 0, VEC)
         gather_scalar(3, 256, 256, 256)
         open_w("w_grouped0")
         grouped[0] = shared.tile([P, 256, PACK], BF16, name="grouped0", offset=64, align_bytes=64)

from contextlib import ExitStack

import concourse.mybir as mybir

K, T, E, C, N = 512, 512, 2, 256, 128
FLOPS = 2 * K * N * E * C

F32 = mybir.dt.float32
BF16 = mybir.dt.bfloat16
U32 = mybir.dt.uint32
U16 = mybir.dt.uint16
U8 = mybir.dt.uint8
FP8X4 = mybir.dt.float8_e4m3fn_x4
GELU = mybir.ActivationFunctionType.Gelu_apprx_tanh
MULT = mybir.AluOpType.mult

P = 128
PACK = 4
SLOTS = E * C
PIECE = 128
COPY = mybir.ActivationFunctionType.Copy
ADD = mybir.AluOpType.add

VEC = 256


def tile_routed_moe_kernel(tc, xT, w, b, gate, offs, out):
    nc = tc.nc
    with ExitStack() as ctx:
        keep = ctx.enter_context(tc.tile_pool(name="keep", bufs=1))
        shared = ctx.enter_context(tc.tile_pool(name="shared", bufs=1))
        psum = ctx.enter_context(tc.psum_pool(name="psum", bufs=1))

        offsets = keep.tile([P, SLOTS // 16], U16, name="offsets")

        x_view = xT.rearrange("(p t) n -> p t n", t=PACK)
        planes = [keep.tile([P, T], F32, name="plane%d" % t) for t in range(PACK)]
        w_raw = [keep.tile([P, PACK, N], F32, name="w_raw%d" % e) for e in range(E)]
        gate_sb = keep.tile([P, SLOTS], F32, name="gate_sb")
        bias = keep.tile([P, E], F32, name="bias")

        def load_plane(t):
            nc.sync.dma_start(planes[t][:], x_view[:, t, :])

        def load_w(e):
            nc.sync.dma_start(w_raw[e][:], w[e].rearrange("(p j) n -> p j n", j=PACK))

        def load_gate():
            nc.sync.dma_start(gate_sb[:], gate)

        def load_bias():
            nc.sync.dma_start(bias[:], b)

        load_plane(0)
        nc.sync.dma_start(offsets[:], offs)
        load_plane(1)
        load_plane(2)
        load_plane(3)
        load_w(0)
        load_bias()
        load_w(1)
        load_gate()

        warm_in = keep.tile([P, 1], F32, name="warm_in")
        warm_out = keep.tile([P, 1], F32, name="warm_out")
        nc.vector.memset(warm_in[:], 0.0)
        nc.scalar.activation(out=warm_out[:], in_=warm_in[:], func=GELU)

        w_grouped = [
            keep.tile([P, N, PACK], BF16, name="w_grouped%d" % e, align_bytes=64) for e in range(0)
        ]
        w_codes = []
        w_scales = [keep.tile([P, N], U8, name="w_scales%d" % e, align_bytes=64) for e in range(E)]
        window = keep.tile([P, T], F32, name="window")
        pairs = keep.tile([P, 2, VEC, 2], BF16, name="pairs", align_bytes=64)
        pair_words = pairs[:].rearrange("p u n e -> p (u n e)").bitcast(F32).rearrange("p (u n) -> p u n", u=2)
        x_bf = [shared.tile([P, T], BF16, name="x_bf0", offset=2048, align_bytes=64)]
        x_bf += [
            keep.tile([P, T], BF16, name="x_bf%d" % t, tag="swap%d" % t, align_bytes=64)
            for t in range(1, PACK)
        ]
        grouped = {}
        x_codes = {}
        x_scales = {}
        results = {}

        def open_w(tag):
            w_grouped.append(
                keep.tile([P, N, PACK], BF16, name="w_grouped%d" % len(w_grouped), tag=tag, align_bytes=64)
            )

        def open_piece(s, count, tag):
            grouped[s] = keep.tile([P, count, PACK], BF16, name="grouped%d" % s, tag=tag, align_bytes=64)

        def open_codes(s, count, tag):
            x_codes[s] = keep.tile([P, count], U32, name="x_codes%d" % s, tag=tag, align_bytes=64)
            x_scales[s] = keep.tile([P, count], U8, name="x_scales%d" % s, align_bytes=64)

        def cast(t, first=0):
            nc.gpsimd.tensor_scalar(
                out=x_bf[t][:, first:], in0=planes[t][:, first:], scalar1=1.0, scalar2=0.0, op0=MULT, op1=ADD
            )

        def gather(t, first, count):
            nc.vector.tensor_copy(
                pairs[:, t // 2, first : first + count, t % 2],
                planes[t][:].indirect(offsets[:, first // 16 : (first + count) // 16]),
            )

        def gather_scalar(t, s, first, count):
            nc.scalar.activation(
                out=grouped[s][:, first - s : first - s + count, t],
                in_=x_bf[t][:].indirect(offsets[:, first // 16 : (first + count) // 16]),
                func=COPY,
            )

        def interleave_vector(s, first, count):
            words = grouped[s][:].rearrange("p n t -> p (n t)").bitcast(F32)
            nc.vector.tensor_copy(
                out=words[:, 2 * (first - s) : 2 * (first - s + count)].rearrange("p (c i u) -> p c u i", i=8, u=2),
                in_=pair_words[:, :, first : first + count].rearrange("p u (c i) -> p c u i", i=8),
            )

        def interleave_w(e):
            nc.scalar.copy(
                out=w_grouped[e][:].rearrange("p (c i) j -> p c j i", i=8),
                in_=w_raw[e][:].rearrange("p j (c i) -> p c j i", i=8),
            )

        def interleave_w_pool(e):
            nc.gpsimd.tensor_scalar(
                out=w_grouped[e][:],
                in0=w_raw[e][:].rearrange("p j n -> p n j"),
                scalar1=1.0,
                scalar2=0.0,
                op0=MULT,
                op1=ADD,
            )

        def interleave_w_vector(e):
            nc.vector.tensor_copy(
                out=w_grouped[e][:].rearrange("p (c i) j -> p c j i", i=8),
                in_=w_raw[e][:].rearrange("p j (c i) -> p c j i", i=8),
            )

        def quantize_w(e):
            nc.vector.quantize_mx(
                out=w_codes[e][:].bitcast(FP8X4),
                scales=w_scales[e][:],
                in_=w_grouped[e][:].rearrange("p n j -> p (n j)"),
            )

        def quantize(s, first, count):
            cols = slice(first - s, first - s + count)
            nc.vector.quantize_mx(
                out=x_codes[s][:, cols].bitcast(FP8X4),
                scales=x_scales[s][:, cols],
                in_=grouped[s][:, cols, :].rearrange("p n t -> p (n t)"),
            )

        def multiply(s, first, count, tag):
            e = first // C
            cols = slice(first - s, first - s + count)
            acc = psum.tile([P, count], F32, name="acc%d" % first)
            nc.tensor.matmul_mx(
                out=acc[:],
                lhsT=w_codes[e][:].bitcast(FP8X4),
                lhsT_scale=w_scales[e][:],
                rhs=x_codes[s][:, cols].bitcast(FP8X4),
                rhs_scale=x_scales[s][:, cols],
                start=True,
                stop=True,
            )
            if s not in results:
                results[s] = keep.tile([P, 256], F32, name="y%d" % s, tag=tag)
            nc.scalar.activation(
                out=results[s][:, cols], in_=acc[:], func=GELU, bias=bias[:, e : e + 1], scale=1.0
            )

        def scatter(first, count):
            nc.vector.tensor_tensor(
                window[:].indirect(offsets[:, first // 16 : (first + count) // 16]),
                results[first][:],
                gate_sb[:, first : first + count],
                MULT,
            )

        open_piece(256, 256, "grouped256")
        nc.scalar.copy(out=x_bf[0][:, : T // 2], in_=planes[0][:, : T // 2])
        cast(0, T // 2)
        gather(0, 0, VEC)
        gather_scalar(0, 256, 256, 256)
        cast(1)
        gather(1, 0, VEC)
        gather_scalar(1, 256, 256, 256)
        cast(2)
        gather(2, 0, VEC)
        gather_scalar(2, 256, 256, 256)
        cast(3)
        gather(3, 0, VEC)
        gather_scalar(3, 256, 256, 256)
        open_w("w_grouped0")
        grouped[0] = shared.tile([P, 256, PACK], BF16, name="grouped0", offset=64, align_bytes=64)
        w_codes.append(shared.tile([P, N], U32, name="w_codes0", offset=2112, align_bytes=64))
        w_codes.append(keep.tile([P, N], U32, name="w_codes1", align_bytes=64))
        w_grouped.append(shared.tile([P, N, PACK], BF16, name="w_grouped1", offset=2624, align_bytes=64))
        open_codes(0, 256, "x_codes0")
        interleave_w_vector(0)
        interleave_vector(0, 0, 128)
        interleave_vector(0, 128, 128)
        quantize_w(0)
        quantize(0, 0, 128)
        quantize(0, 128, 128)
        multiply(0, 0, 128, "plane3")
        multiply(0, 128, 128, "plane3")
        interleave_w_vector(1)
        open_codes(256, 256, "x_codes256")
        quantize(256, 256, 256)
        quantize_w(1)
        multiply(256, 256, 256, "y256")
        scatter(0, 256)
        scatter(256, 256)

        nc.sync.dma_start(out, window[:])
